import numpy as np
import ml_dtypes


def mxq(x, axis, fmt="e4m3"):
    dtype, down = {"e4m3": (ml_dtypes.float8_e4m3fn, 7), "e5m2": (ml_dtypes.float8_e5m2, 14)}[fmt]
    v = np.moveaxis(np.asarray(x, np.float32).astype(ml_dtypes.bfloat16).astype(np.float64), axis, -1)
    blocks = v.reshape(v.shape[:-1] + (-1, 32))
    amax = np.abs(blocks).max(-1, keepdims=True)
    byte = np.maximum(np.where(amax > 0, np.frexp(amax)[1] - 1 + 127, 0) - down, 1)
    scale = np.exp2(byte - 127.0)
    codes = (blocks / scale).astype(np.float32).astype(dtype).astype(np.float64)
    return np.moveaxis((codes * scale).reshape(v.shape), -1, axis)


WIDE = False


def mx_kscale(k):
    if not WIDE:
        return np.ones(k)
    levels = np.array([30, -30])
    if k % 512:
        return np.exp2(np.random.permutation(np.resize(levels, k // 32))).repeat(32)
    a = np.empty((k // 512, 16))
    for p in range(k // 512):
        a[p, :8] = np.random.permutation(np.resize(levels, 8))
        for g in range(8):
            far = levels[np.abs(levels - a[p, g]) >= 10]
            a[p, g + 8] = far[np.random.randint(len(far))]
    return np.exp2(a.ravel()).repeat(32)


def f64(x):
    return np.asarray(x).astype(np.float64)


def striped8(idx):
    return np.asarray(idx).reshape(8, -1, 16).transpose(0, 2, 1).reshape(128, -1).astype(np.uint16)


def unstriped8(offs):
    return offs.reshape(8, 16, -1).transpose(0, 2, 1).reshape(8, -1).astype(np.int64)


def pick8(x, idx, run):
    r = np.arange(len(x))
    return x[r[:, None], idx[r % (8 * run) // run]]


E2M1 = np.array([0.0, 0.5, 1.0, 1.5, 2.0, 3.0, 4.0, 6.0, -0.0, -0.5, -1.0, -1.5, -2.0, -3.0, -4.0, -6.0])


def pack_weight(w, fmt):
    k, n = w.shape
    w = f64(np.asarray(w, np.float32).astype(ml_dtypes.bfloat16)).reshape(k // 32, 32, n)
    amax = np.abs(w).max(1)
    if fmt in ("e4m3", "e5m2"):
        byte = np.frexp(amax)[1] - 1 + 127 - (7 if fmt == "e4m3" else 14)
    else:
        mant, ex = np.frexp(amax / 6.0)
        byte = np.where(mant > 0.5, ex, ex - 1) + 127
    byte = np.clip(np.where(amax > 0, byte, 1), 1, 254)
    scaled = (w * np.exp2(127.0 - byte)[:, None, :]).reshape(k, n).astype(np.float32)
    by_word = np.ascontiguousarray(scaled.reshape(k // 512, 128, 4, n).transpose(0, 1, 3, 2))
    if fmt in ("e4m3", "e5m2"):
        words = by_word.astype(ml_dtypes.float8_e4m3fn if fmt == "e4m3" else ml_dtypes.float8_e5m2).view(np.uint8)
    else:
        c = by_word.astype(ml_dtypes.float4_e2m1fn).view(np.uint8) & 0xF
        words = (c[..., 0::2] | (c[..., 1::2] << 4)).reshape(k // 512, 128, 2 * n)
    return np.ascontiguousarray(words), np.ascontiguousarray(byte.astype(np.uint8).reshape(k // 512, 16, n))


def unpack_weight(words, scales, fmt):
    g, _, n = scales.shape
    words = np.ascontiguousarray(words).reshape(g, 128, n, -1)
    if fmt in ("e4m3", "e5m2"):
        vals = words.view(ml_dtypes.float8_e4m3fn if fmt == "e4m3" else ml_dtypes.float8_e5m2).astype(np.float64)
    else:
        nib = np.empty((g, 128, n, 4), np.uint8)
        nib[..., 0::2] = words & 0xF
        nib[..., 1::2] = words >> 4
        vals = E2M1[nib]
    vals = vals * np.repeat(np.exp2(scales.astype(np.float64) - 127.0), 8, axis=1)[..., None]
    return vals.transpose(0, 1, 3, 2).reshape(g * 512, n)


def bf(x):
    return np.asarray(x, np.float32).astype(ml_dtypes.bfloat16)


def planes(Y):
    r, m = Y.shape
    b = f64(bf(Y)).reshape(r // 32, 32, m)
    amax = np.abs(b).max(1)
    byte = np.clip(np.where(amax > 0, np.frexp(amax)[1] - 1 + 127 - 7, 1), 1, 254)
    codes = (b * np.exp2(127.0 - byte)[:, None, :]).reshape(r, m).astype(np.float32).astype(ml_dtypes.float8_e4m3fn).view(np.uint8)
    words = codes.reshape(r // 512, 128, 4, m).transpose(0, 1, 3, 2)
    return np.ascontiguousarray(words), np.ascontiguousarray(byte.astype(np.uint8).reshape(r // 512, 16, m))


K, J, N, T = 512, 512, 256, 1024


def setup_inputs():
    n = np.random.standard_normal
    idx = np.stack([np.random.permutation(T)[:J] for _ in range(8)])
    fj = mx_kscale(J)
    gjp = pack_weight(n((J, N)) * np.exp(0.5 * n((J, 1))) / fj[:, None], "e5m2")
    return {
        "xf": (n((K, T))).astype(np.float32),
        "ra": (np.random.uniform(0.5, 1.5, (1, J)) * fj).astype(np.float32),
        "gj_words": gjp[0],
        "gj_scales": gjp[1],
        "old": (1.0 * n((K, N))).astype(np.float32),
        "offs": striped8(idx),
    }


def reference(xf, ra, gj_words, gj_scales, old, offs):
    idx = unstriped8(offs)
    gju = unpack_weight(gj_words, gj_scales, "e5m2")
    us = pick8(f64(xf), idx, 64) * f64(ra)
    uj = us.T
    ujq = mxq(uj, 0, "e5m2")
    w = ujq.T @ gju
    pk1 = np.max(np.abs(w), axis=1, keepdims=True)
    y = w / (pk1 + 2.0) - 0.3 * f64(old)
    words, scales = planes(y)
    return y, words, scales

@@ -1,0 +1,153 @@
+from contextlib import ExitStack
+
+import concourse.mybir as mybir
+from concourse.masks import make_identity
+
+K, J, N, T = 512, 512, 256, 1024
+FLOPS = 2 * K * J * N
+
+F32 = mybir.dt.float32
+BF16 = mybir.dt.bfloat16
+I32 = mybir.dt.int32
+U32 = mybir.dt.uint32
+U16 = mybir.dt.uint16
+U8 = mybir.dt.uint8
+E5M2X4 = mybir.dt.float8_e5m2_x4
+E4M3X4 = mybir.dt.float8_e4m3fn_x4
+ALU = mybir.AluOpType
+ACT = mybir.ActivationFunctionType
+
+P = 128
+PACK = 4
+
+
+def tile_list_moment_headpicks_stored_rowpeaks_pl_kernel(tc, xf, ra, gj_words, gj_scales, old, offs, out_0, out_1, out_2):
+    nc = tc.nc
+    with ExitStack() as ctx:
+        keep = ctx.enter_context(tc.tile_pool(name="keep", bufs=1))
+        psum = ctx.enter_context(tc.psum_pool(name="psum", bufs=1))
+        turn = ctx.enter_context(tc.psum_pool(name="turn", bufs=3))
+
+        offsets = keep.tile([P, J // 16], U16, name="offsets")
+        nc.sync.dma_start(offsets[:], offs)
+
+        xf_rows = xf.rearrange("(p t) c -> p t c", t=PACK)
+        x = [keep.tile([P, T], F32, name="x%d" % t) for t in range(PACK)]
+        ra4 = keep.tile([P, PACK], F32, name="ra4")
+        g_words = keep.tile([P, N], U32, name="g_words", align_bytes=64)
+        g_scales = keep.tile([P, N], U8, name="g_scales", align_bytes=64)
+        old_sb = keep.tile([P, PACK, N], F32, name="old_sb")
+        nc.sync.dma_start(x[0][:], xf_rows[:, 0, :])
+        nc.sync.dma_start(ra4[:], ra.rearrange("o (q s) -> (o q) s", s=PACK))
+        nc.sync.dma_start(x[1][:], xf_rows[:, 1, :])
+        nc.sync.dma_start(g_words[:].bitcast(I32), gj_words[0].rearrange("p n r -> p (n r)").bitcast(I32))
+        nc.sync.dma_start(x[2][:], xf_rows[:, 2, :])
+        nc.sync.dma_start(x[3][:], xf_rows[:, 3, :])
+        nc.sync.dma_start(old_sb[:], old.rearrange("(p t) n -> p t n", t=PACK))
+
+        nc.gpsimd.memset(g_scales[:].bitcast(I32), 0)
+        ident = keep.tile([P, P], F32, name="ident")
+        make_identity(nc, ident[:])
+        for quad in range(4):
+            nc.gpsimd.dma_start(
+                g_scales[32 * quad : 32 * quad + 4, :].bitcast(I32),
+                gj_scales[0, 4 * quad : 4 * quad + 4, :].bitcast(I32),
+            )
+
+        ra_all = psum.tile([P, PACK, P], F32, name="ra_all")
+        for s in range(PACK):
+            nc.tensor.transpose(ra_all[:, s, :], ra4[:, s : s + 1].to_broadcast([P, P]), ident[:])
+
+        picked = [keep.tile([P, J], F32, name="picked%d" % t) for t in range(PACK)]
+        pairs = [keep.tile([P, 2, P, 2], BF16, name="pairs%d" % t) for t in range(PACK)]
+        grouped = [keep.tile([P, P, PACK], BF16, name="grouped%d" % t, align_bytes=64) for t in range(PACK)]
+        u_codes = [keep.tile([P, P], U32, name="u_codes%d" % t, align_bytes=64) for t in range(PACK)]
+        u_scales = [keep.tile([P, P], U8, name="u_scales%d" % t, align_bytes=64) for t in range(PACK)]
+        w = [psum.tile([P, N], F32, name="w%d" % t) for t in range(PACK)]
+        mag = [keep.tile([P, N], F32, name="mag%d" % t) for t in range(PACK)]
+        shifted = keep.tile([P, N], F32, name="shifted")
+        denom = [keep.tile([P, 1], F32, name="denom%d" % t) for t in range(PACK)]
+        inv = [keep.tile([P, 1], F32, name="inv%d" % t) for t in range(PACK)]
+        old_part = [keep.tile([P, N], F32, name="old_part%d" % t) for t in range(PACK)]
+        y = keep.tile([P, PACK, N], F32, name="y")
+        out_rows = out_0.rearrange("(p t) n -> p t n", t=PACK)
+
+        def gather(t):
+            if t == 0:
+                half = J // 2
+                nc.vector.tensor_copy(picked[t][:, :half], x[t][:].indirect(offsets[:, : half // 16]))
+                nc.scalar.activation(picked[t][:, half:], x[t][:].indirect(offsets[:, half // 16 :]), ACT.Copy)
+            else:
+                nc.scalar.activation(picked[t][:], x[t][:].indirect(offsets[:]), ACT.Copy)
+
+        def weigh(t):
+            nc.vector.tensor_tensor(
+                pairs[t][:],
+                picked[t][:].rearrange("p (q u e) -> p u q e", u=2, e=2),
+                ra_all[:].rearrange("p (u e) q -> p u q e", u=2),
+                ALU.mult,
+            )
+
+        def turn_over(t):
+            words = pairs[t][:].rearrange("p u q e -> p (u q e)").bitcast(F32)
+            turned = turn.tile([P, 2, P], F32, name="turned")
+            for u in range(2):
+                nc.tensor.transpose(turned[:, u, :], words[:, u * P : (u + 1) * P], ident[:])
+            dst = grouped[t][:].rearrange("q p s -> q (p s)").bitcast(F32).rearrange("q (p u) -> q p u", u=2)
+            if t == 0:
+                nc.vector.tensor_copy(dst, turned[:].rearrange("q u p -> q p u"))
+            else:
+                nc.scalar.copy(dst, turned[:].rearrange("q u p -> q p u"))
+
+        def product(t):
+            nc.vector.quantize_mx(
+                out=u_codes[t][:].bitcast(E5M2X4),
+                scales=u_scales[t][:],
+                in_=grouped[t][:].rearrange("q p s -> q (p s)"),
+            )
+            nc.tensor.matmul_mx(
+                out=w[t][:],
+                lhsT=u_codes[t][:].bitcast(E5M2X4),
+                lhsT_scale=u_scales[t][:],
+                rhs=g_words[:].bitcast(E5M2X4),
+                rhs_scale=g_scales[:],
+                start=True,
+                stop=True,
+            )
+
+        def peak(t):
+            nc.scalar.activation(mag[t][:], w[t][:], ACT.Abs)
+            nc.vector.tensor_scalar(shifted[:], mag[t][:], 2.0, None, ALU.add, ALU.max, accum_out=denom[t][:])
+            nc.vector.reciprocal(inv[t][:], denom[t][:])
+
+        def finish(t):
+            nc.gpsimd.tensor_scalar(old_part[t][:], old_sb[:, t, :], -0.3, 0.0, ALU.mult, ALU.add)
+            nc.vector.scalar_tensor_tensor(y[:, t, :], w[t][:], inv[t][:], old_part[t][:], ALU.mult, ALU.add)
+            nc.sync.dma_start(out_rows[:, t, :], y[:, t, :])
+
+        stages = [gather, weigh, turn_over, product, peak, finish]
+        for step in range(PACK + len(stages) - 1):
+            for depth in range(len(stages)):
+                t = step - depth
+                if 0 <= t < PACK:
+                    stages[depth](t)
+
+        y_grouped = keep.tile([P, N, PACK], BF16, name="y_grouped", align_bytes=64)
+        nc.vector.tensor_copy(
+            y_grouped[:].rearrange("p (c i) t -> p c t i", i=4),
+            y[:].rearrange("p t (c i) -> p c t i", i=4),
+        )
+        y_codes = keep.tile([P, N], U32, name="y_codes", align_bytes=64)
+        y_scales = keep.tile([P, N], U8, name="y_scales", align_bytes=64)
+        nc.vector.quantize_mx(
+            out=y_codes[:].bitcast(E4M3X4),
+            scales=y_scales[:],
+            in_=y_grouped[:].rearrange("p n t -> p (n t)"),
+        )
+        nc.sync.dma_start(out_1[0].rearrange("p n r -> p (n r)").bitcast(I32), y_codes[:].bitcast(I32))
+        for quad in range(4):
+            queue = nc.scalar if quad % 2 == 0 else nc.sync
+            queue.dma_start(
+                out_2[0, 4 * quad : 4 * quad + 4, :].bitcast(I32),
+                y_scales[32 * quad : 32 * quad + 4, :].bitcast(I32),
+            )

@@ -37,77 +37,71 @@ def tile_list_moment_headpicks_stored_rowpeaks_pl_kernel(tc, xf, ra, gj_words, g
         g_words = keep.tile([P, N], U32, name="g_words", align_bytes=64)
         g_scales = keep.tile([P, N], U8, name="g_scales", align_bytes=64)
         old_sb = keep.tile([P, PACK, N], F32, name="old_sb")
-        nc.sync.dma_start(x[0][:], xf_rows[:, 0, :])
-        nc.sync.dma_start(ra4[:], ra.rearrange("o (q s) -> (o q) s", s=PACK))
-        nc.sync.dma_start(x[1][:], xf_rows[:, 1, :])
-        nc.sync.dma_start(g_words[:].bitcast(I32), gj_words[0].rearrange("p n r -> p (n r)").bitcast(I32))
-        nc.sync.dma_start(x[2][:], xf_rows[:, 2, :])
-        nc.sync.dma_start(x[3][:], xf_rows[:, 3, :])
-        nc.sync.dma_start(old_sb[:], old.rearrange("(p t) n -> p t n", t=PACK))
-
         nc.gpsimd.memset(g_scales[:].bitcast(I32), 0)
-        ident = keep.tile([P, P], F32, name="ident")
-        make_identity(nc, ident[:])
+        nc.scalar.dma_start(ra4[:], ra.rearrange("o (q s) -> (o q) s", s=PACK))
+        for t in range(PACK):
+            nc.sync.dma_start(x[t][:], xf_rows[:, t, :])
+        nc.sync.dma_start(g_words[:].bitcast(I32), gj_words[0].rearrange("p n r -> p (n r)").bitcast(I32))
         for quad in range(4):
-            nc.gpsimd.dma_start(
+            nc.sync.dma_start(
                 g_scales[32 * quad : 32 * quad + 4, :].bitcast(I32),
                 gj_scales[0, 4 * quad : 4 * quad + 4, :].bitcast(I32),
             )
+        nc.sync.dma_start(old_sb[:], old.rearrange("(p t) n -> p t n", t=PACK))
+
+        ident = keep.tile([P, P], F32, name="ident")
+        make_identity(nc, ident[:])
+        one = keep.tile([P, 1], F32, name="one")
+        two = keep.tile([P, 1], F32, name="two")
+        nc.gpsimd.memset(one[:], 1.0)
+        nc.scalar.activation(two[:], one[:], ACT.Abs, scale=2.0)
 
         ra_all = psum.tile([P, PACK, P], F32, name="ra_all")
         for s in range(PACK):
             nc.tensor.transpose(ra_all[:, s, :], ra4[:, s : s + 1].to_broadcast([P, P]), ident[:])
 
-        picked = [keep.tile([P, J], F32, name="picked%d" % t) for t in range(PACK)]
-        pairs = [keep.tile([P, 2, P, 2], BF16, name="pairs%d" % t) for t in range(PACK)]
-        grouped = [keep.tile([P, P, PACK], BF16, name="grouped%d" % t, align_bytes=64) for t in range(PACK)]
-        u_codes = [keep.tile([P, P], U32, name="u_codes%d" % t, align_bytes=64) for t in range(PACK)]
+        half = J // 2
+        last = PACK - 1
+        picked0 = keep.tile([P, J], F32, name="picked0")
+        picked1_hi = keep.tile([P, half], F32, name="picked1_hi")
+        picked2 = keep.tile([P, J], F32, name="picked2")
+        picked3_lo = keep.tile([P, half], F32, name="picked3_lo")
+        picked3_hi = keep.tile([P, half], F32, name="picked3_hi", align_bytes=64)
         u_scales = [keep.tile([P, P], U8, name="u_scales%d" % t, align_bytes=64) for t in range(PACK)]
         w = [psum.tile([P, N], F32, name="w%d" % t) for t in range(PACK)]
-        mag = [keep.tile([P, N], F32, name="mag%d" % t) for t in range(PACK)]
         shifted = keep.tile([P, N], F32, name="shifted")
         denom = [keep.tile([P, 1], F32, name="denom%d" % t) for t in range(PACK)]
         inv = [keep.tile([P, 1], F32, name="inv%d" % t) for t in range(PACK)]
-        old_part = [keep.tile([P, N], F32, name="old_part%d" % t) for t in range(PACK)]
         y = keep.tile([P, PACK, N], F32, name="y")
         out_rows = out_0.rearrange("(p t) n -> p t n", t=PACK)
+        lo_list = offsets[:, : half // 16]
+        hi_list = offsets[:, half // 16 :]
 
-        def gather(t):
-            if t == 0:
-                half = J // 2
-                nc.vector.tensor_copy(picked[t][:, :half], x[t][:].indirect(offsets[:, : half // 16]))
-                nc.scalar.activation(picked[t][:, half:], x[t][:].indirect(offsets[:, half // 16 :]), ACT.Copy)
-            else:
-                nc.scalar.activation(picked[t][:], x[t][:].indirect(offsets[:]), ACT.Copy)
-
-        def weigh(t):
+        def weigh(pairs, values, q0, q1):
             nc.vector.tensor_tensor(
-                pairs[t][:],
-                picked[t][:].rearrange("p (q u e) -> p u q e", u=2, e=2),
-                ra_all[:].rearrange("p (u e) q -> p u q e", u=2),
+                pairs[:, :, q0:q1, :],
+                values.rearrange("p (q u e) -> p u q e", u=2, e=2),
+                ra_all[:].rearrange("p (u e) q -> p u q e", u=2)[:, :, q0:q1, :],
                 ALU.mult,
             )
 
-        def turn_over(t):
-            words = pairs[t][:].rearrange("p u q e -> p (u q e)").bitcast(F32)
+        def turn_over(pairs, grouped, copy):
+            words = pairs[:].rearrange("p u q e -> p (u q e)").bitcast(F32)
             turned = turn.tile([P, 2, P], F32, name="turned")
             for u in range(2):
                 nc.tensor.transpose(turned[:, u, :], words[:, u * P : (u + 1) * P], ident[:])
-            dst = grouped[t][:].rearrange("q p s -> q (p s)").bitcast(F32).rearrange("q (p u) -> q p u", u=2)
-            if t == 0:
-                nc.vector.tensor_copy(dst, turned[:].rearrange("q u p -> q p u"))
-            else:
-                nc.scalar.copy(dst, turned[:].rearrange("q u p -> q p u"))
+            dst = grouped[:].rearrange("q p s -> q (p s)").bitcast(F32).rearrange("q (p u) -> q p u", u=2)
+            copy(dst, turned[:].rearrange("q u p -> q p u"))
 
-        def product(t):
+        def product(t, grouped, codes):
             nc.vector.quantize_mx(
-                out=u_codes[t][:].bitcast(E5M2X4),
+                out=codes.bitcast(E5M2X4),
                 scales=u_scales[t][:],
-                in_=grouped[t][:].rearrange("q p s -> q (p s)"),
+                in_=grouped[:].rearrange("q p s -> q (p s)"),
             )
             nc.tensor.matmul_mx(
                 out=w[t][:],
-                lhsT=u_codes[t][:].bitcast(E5M2X4),
+                lhsT=codes.bitcast(E5M2X4),
                 lhsT_scale=u_scales[t][:],
                 rhs=g_words[:].bitcast(E5M2X4),
                 rhs_scale=g_scales[:],
@@ -115,27 +109,72 @@ def tile_list_moment_headpicks_stored_rowpeaks_pl_kernel(tc, xf, ra, gj_words, g
                 stop=True,
             )
 
-        def peak(t):
-            nc.scalar.activation(mag[t][:], w[t][:], ACT.Abs)
-            nc.vector.tensor_scalar(shifted[:], mag[t][:], 2.0, None, ALU.add, ALU.max, accum_out=denom[t][:])
+        def peak(t, mag):
+            nc.scalar.activation(mag, w[t][:], ACT.Abs)
+            nc.vector.tensor_scalar(shifted[:], mag, two[:], None, ALU.add, ALU.max, accum_out=denom[t][:])
             nc.vector.reciprocal(inv[t][:], denom[t][:])
 
-        def finish(t):
-            nc.gpsimd.tensor_scalar(old_part[t][:], old_sb[:, t, :], -0.3, 0.0, ALU.mult, ALU.add)
-            nc.vector.scalar_tensor_tensor(y[:, t, :], w[t][:], inv[t][:], old_part[t][:], ALU.mult, ALU.add)
+        def finish(t, part):
+            nc.scalar.activation(part, old_sb[:, t, :], ACT.Copy, scale=-0.3)
+            nc.vector.scalar_tensor_tensor(y[:, t, :], w[t][:], inv[t][:], part, ALU.mult, ALU.add)
             nc.sync.dma_start(out_rows[:, t, :], y[:, t, :])
 
-        stages = [gather, weigh, turn_over, product, peak, finish]
-        for step in range(PACK + len(stages) - 1):
-            for depth in range(len(stages)):
-                t = step - depth
-                if 0 <= t < PACK:
-                    stages[depth](t)
+        def pair_tile(t, tag):
+            return keep.tile([P, 2, P, 2], BF16, name="pairs%d" % t, tag=tag, align_bytes=64)
+
+        grouped = [keep.tile([P, P, PACK], BF16, name="grouped%d" % t, align_bytes=64) for t in range(PACK)]
+
+        nc.vector.tensor_copy(picked0[:, :half], x[0][:].indirect(lo_list))
+        nc.scalar.activation(picked0[:, half:], x[0][:].indirect(hi_list), ACT.Copy)
+        nc.scalar.activation(picked1_hi[:], x[1][:].indirect(hi_list), ACT.Copy)
+        nc.scalar.activation(picked2[:], x[2][:].indirect(offsets[:]), ACT.Copy)
+        nc.scalar.activation(picked3_lo[:], x[3][:].indirect(lo_list), ACT.Copy)
+        nc.scalar.activation(picked3_hi[:], x[3][:].indirect(hi_list), ACT.Copy)
+
+        pairs0 = pair_tile(0, "pairs0")
+        weigh(pairs0, picked0[:], 0, P)
+        picked1_lo = keep.tile([P, half], F32, name="picked1_lo", tag="picked0")
+        nc.vector.tensor_copy(picked1_lo[:], x[1][:].indirect(lo_list))
+        pairs1 = pair_tile(1, "pairs1")
+        weigh(pairs1, picked1_hi[:], P // 2, P)
+        weigh(pairs1, picked1_lo[:], 0, P // 2)
+        turn_over(pairs0, grouped[0], nc.vector.tensor_copy)
+        pairs2 = pair_tile(2, "pairs0")
+        weigh(pairs2, picked2[:], 0, P)
+        turn_over(pairs1, grouped[1], nc.scalar.copy)
+        pairs3 = pair_tile(3, "pairs1")
+        weigh(pairs3, picked3_lo[:], 0, P // 2)
+        codes0 = keep.tile([P, P], U32, name="codes0", align_bytes=64)
+        product(0, grouped[0], codes0[:])
+        weigh(pairs3, picked3_hi[:], P // 2, P)
+        turn_over(pairs2, grouped[2], nc.scalar.copy)
+        turn_over(pairs3, grouped[3], nc.scalar.copy)
+        codes3 = keep.tile([P, P], U32, name="codes3", align_bytes=64)
+        product(3, grouped[3], codes3[:])
+        codes12 = keep.tile([P, 2, P], U32, name="codes12", tag="picked3_hi", align_bytes=64)
+        product(1, grouped[1], codes12[:, 0, :])
+        product(2, grouped[2], codes12[:, 1, :])
+
+        early = keep.tile([P, 3, N], F32, name="early", tag="picked3_lo")
+        late = keep.tile([P, 4, N], F32, name="late", tag="pairs1", align_bytes=64)
+        mag3 = keep.tile([P, N], F32, name="mag3")
+        peak(0, early[:, 0, :])
+        peak(1, early[:, 1, :])
+        peak(2, late[:, 0, :])
+        peak(3, mag3[:])
+        finish(0, early[:, 2, :])
+        for t in range(1, PACK):
+            finish(t, late[:, t, :])
 
         y_grouped = keep.tile([P, N, PACK], BF16, name="y_grouped", align_bytes=64)
+        split = 192
         nc.vector.tensor_copy(
-            y_grouped[:].rearrange("p (c i) t -> p c t i", i=4),
-            y[:].rearrange("p t (c i) -> p c t i", i=4),
+            y_grouped[:, :split, :].rearrange("p (c i) t -> p c t i", i=4),
+            y[:, :, :split].rearrange("p t (c i) -> p c t i", i=4),
+        )
+        nc.scalar.copy(
+            y_grouped[:, split:, :],
+            y[:, :, split:].rearrange("p t n -> p n t"),
         )
         y_codes = keep.tile([P, N], U32, name="y_codes", align_bytes=64)
         y_scales = keep.tile([P, N], U8, name="y_scales", align_bytes=64)

@@ -39,14 +39,15 @@ def tile_list_moment_headpicks_stored_rowpeaks_pl_kernel(tc, xf, ra, gj_words, g
         old_sb = keep.tile([P, PACK, N], F32, name="old_sb")
         nc.gpsimd.memset(g_scales[:].bitcast(I32), 0)
         nc.scalar.dma_start(ra4[:], ra.rearrange("o (q s) -> (o q) s", s=PACK))
-        for t in range(PACK):
-            nc.sync.dma_start(x[t][:], xf_rows[:, t, :])
-        nc.sync.dma_start(g_words[:].bitcast(I32), gj_words[0].rearrange("p n r -> p (n r)").bitcast(I32))
+        nc.sync.dma_start(x[0][:], xf_rows[:, 0, :])
         for quad in range(4):
             nc.sync.dma_start(
                 g_scales[32 * quad : 32 * quad + 4, :].bitcast(I32),
                 gj_scales[0, 4 * quad : 4 * quad + 4, :].bitcast(I32),
             )
+        for t in range(1, PACK):
+            nc.sync.dma_start(x[t][:], xf_rows[:, t, :])
+        nc.sync.dma_start(g_words[:].bitcast(I32), gj_words[0].rearrange("p n r -> p (n r)").bitcast(I32))
         nc.sync.dma_start(old_sb[:], old.rearrange("(p t) n -> p t n", t=PACK))
 
         ident = keep.tile([P, P], F32, name="ident")
@@ -167,7 +168,7 @@ def tile_list_moment_headpicks_stored_rowpeaks_pl_kernel(tc, xf, ra, gj_words, g
             finish(t, late[:, t, :])
 
         y_grouped = keep.tile([P, N, PACK], BF16, name="y_grouped", align_bytes=64)
-        split = 192
+        split = 144
         nc.vector.tensor_copy(
             y_grouped[:, :split, :].rearrange("p (c i) t -> p c t i", i=4),
             y[:, :, :split].rearrange("p t (c i) -> p c t i", i=4),

@@ -19,6 +19,12 @@ ACT = mybir.ActivationFunctionType
 
 P = 128
 PACK = 4
+QUADS = 4
+GROUP = 16
+HALF = J // 2
+OLD_FACTOR = -0.3
+PEAK_SHIFT = 2.0
+VECTOR_COLUMNS = 192
 
 
 def tile_list_moment_headpicks_stored_rowpeaks_pl_kernel(tc, xf, ra, gj_words, gj_scales, old, offs, out_0, out_1, out_2):
@@ -28,8 +34,7 @@ def tile_list_moment_headpicks_stored_rowpeaks_pl_kernel(tc, xf, ra, gj_words, g
         psum = ctx.enter_context(tc.psum_pool(name="psum", bufs=1))
         turn = ctx.enter_context(tc.psum_pool(name="turn", bufs=3))
 
-        offsets = keep.tile([P, J // 16], U16, name="offsets")
-        nc.sync.dma_start(offsets[:], offs)
+        offsets = keep.tile([P, J // GROUP], U16, name="offsets")
 
         xf_rows = xf.rearrange("(p t) c -> p t c", t=PACK)
         x = [keep.tile([P, T], F32, name="x%d" % t) for t in range(PACK)]
@@ -40,43 +45,41 @@ def tile_list_moment_headpicks_stored_rowpeaks_pl_kernel(tc, xf, ra, gj_words, g
         nc.gpsimd.memset(g_scales[:].bitcast(I32), 0)
         nc.scalar.dma_start(ra4[:], ra.rearrange("o (q s) -> (o q) s", s=PACK))
         nc.sync.dma_start(x[0][:], xf_rows[:, 0, :])
-        for quad in range(4):
+        nc.sync.dma_start(offsets[:], offs)
+        for t in range(1, PACK):
+            nc.sync.dma_start(x[t][:], xf_rows[:, t, :])
+        nc.sync.dma_start(g_words[:].bitcast(I32), gj_words[0].rearrange("p n r -> p (n r)").bitcast(I32))
+        for quad in range(QUADS):
             nc.sync.dma_start(
                 g_scales[32 * quad : 32 * quad + 4, :].bitcast(I32),
                 gj_scales[0, 4 * quad : 4 * quad + 4, :].bitcast(I32),
             )
-        for t in range(1, PACK):
-            nc.sync.dma_start(x[t][:], xf_rows[:, t, :])
-        nc.sync.dma_start(g_words[:].bitcast(I32), gj_words[0].rearrange("p n r -> p (n r)").bitcast(I32))
         nc.sync.dma_start(old_sb[:], old.rearrange("(p t) n -> p t n", t=PACK))
 
         ident = keep.tile([P, P], F32, name="ident")
         make_identity(nc, ident[:])
         one = keep.tile([P, 1], F32, name="one")
-        two = keep.tile([P, 1], F32, name="two")
+        shift = keep.tile([P, 1], F32, name="shift")
         nc.gpsimd.memset(one[:], 1.0)
-        nc.scalar.activation(two[:], one[:], ACT.Abs, scale=2.0)
+        nc.scalar.activation(shift[:], one[:], ACT.Abs, scale=PEAK_SHIFT)
 
         ra_all = psum.tile([P, PACK, P], F32, name="ra_all")
         for s in range(PACK):
             nc.tensor.transpose(ra_all[:, s, :], ra4[:, s : s + 1].to_broadcast([P, P]), ident[:])
 
-        half = J // 2
-        last = PACK - 1
         picked0 = keep.tile([P, J], F32, name="picked0")
-        picked1_hi = keep.tile([P, half], F32, name="picked1_hi")
+        picked1_hi = keep.tile([P, HALF], F32, name="picked1_hi")
         picked2 = keep.tile([P, J], F32, name="picked2")
-        picked3_lo = keep.tile([P, half], F32, name="picked3_lo")
-        picked3_hi = keep.tile([P, half], F32, name="picked3_hi", align_bytes=64)
+        picked3_lo = keep.tile([P, HALF], F32, name="picked3_lo")
+        picked3_hi = keep.tile([P, HALF], F32, name="picked3_hi", align_bytes=64)
         u_scales = [keep.tile([P, P], U8, name="u_scales%d" % t, align_bytes=64) for t in range(PACK)]
         w = [psum.tile([P, N], F32, name="w%d" % t) for t in range(PACK)]
-        shifted = keep.tile([P, N], F32, name="shifted")
         denom = [keep.tile([P, 1], F32, name="denom%d" % t) for t in range(PACK)]
         inv = [keep.tile([P, 1], F32, name="inv%d" % t) for t in range(PACK)]
         y = keep.tile([P, PACK, N], F32, name="y")
         out_rows = out_0.rearrange("(p t) n -> p t n", t=PACK)
-        lo_list = offsets[:, : half // 16]
-        hi_list = offsets[:, half // 16 :]
+        lo_list = offsets[:, : HALF // GROUP]
+        hi_list = offsets[:, HALF // GROUP :]
 
         def weigh(pairs, values, q0, q1):
             nc.vector.tensor_tensor(
@@ -112,11 +115,11 @@ def tile_list_moment_headpicks_stored_rowpeaks_pl_kernel(tc, xf, ra, gj_words, g
 
         def peak(t, mag):
             nc.scalar.activation(mag, w[t][:], ACT.Abs)
-            nc.vector.tensor_scalar(shifted[:], mag, two[:], None, ALU.add, ALU.max, accum_out=denom[t][:])
+            nc.vector.tensor_scalar(mag, mag, shift[:], None, ALU.add, ALU.max, accum_out=denom[t][:])
             nc.vector.reciprocal(inv[t][:], denom[t][:])
 
         def finish(t, part):
-            nc.scalar.activation(part, old_sb[:, t, :], ACT.Copy, scale=-0.3)
+            nc.scalar.activation(part, old_sb[:, t, :], ACT.Copy, scale=OLD_FACTOR)
             nc.vector.scalar_tensor_tensor(y[:, t, :], w[t][:], inv[t][:], part, ALU.mult, ALU.add)
             nc.sync.dma_start(out_rows[:, t, :], y[:, t, :])
 
@@ -125,8 +128,8 @@ def tile_list_moment_headpicks_stored_rowpeaks_pl_kernel(tc, xf, ra, gj_words, g
 
         grouped = [keep.tile([P, P, PACK], BF16, name="grouped%d" % t, align_bytes=64) for t in range(PACK)]
 
-        nc.vector.tensor_copy(picked0[:, :half], x[0][:].indirect(lo_list))
-        nc.scalar.activation(picked0[:, half:], x[0][:].indirect(hi_list), ACT.Copy)
+        nc.vector.tensor_copy(picked0[:, :HALF], x[0][:].indirect(lo_list))
+        nc.scalar.activation(picked0[:, HALF:], x[0][:].indirect(hi_list), ACT.Copy)
         nc.scalar.activation(picked1_hi[:], x[1][:].indirect(hi_list), ACT.Copy)
         nc.scalar.activation(picked2[:], x[2][:].indirect(offsets[:]), ACT.Copy)
         nc.scalar.activation(picked3_lo[:], x[3][:].indirect(lo_list), ACT.Copy)
@@ -134,7 +137,7 @@ def tile_list_moment_headpicks_stored_rowpeaks_pl_kernel(tc, xf, ra, gj_words, g
 
         pairs0 = pair_tile(0, "pairs0")
         weigh(pairs0, picked0[:], 0, P)
-        picked1_lo = keep.tile([P, half], F32, name="picked1_lo", tag="picked0")
+        picked1_lo = keep.tile([P, HALF], F32, name="picked1_lo", tag="picked0")
         nc.vector.tensor_copy(picked1_lo[:], x[1][:].indirect(lo_list))
         pairs1 = pair_tile(1, "pairs1")
         weigh(pairs1, picked1_hi[:], P // 2, P)
@@ -157,25 +160,25 @@ def tile_list_moment_headpicks_stored_rowpeaks_pl_kernel(tc, xf, ra, gj_words, g
         product(2, grouped[2], codes12[:, 1, :])
 
         early = keep.tile([P, 3, N], F32, name="early", tag="picked3_lo")
-        late = keep.tile([P, 4, N], F32, name="late", tag="pairs1", align_bytes=64)
+        mag2 = keep.tile([P, N], F32, name="mag2", tag="pairs1", align_bytes=64)
         mag3 = keep.tile([P, N], F32, name="mag3")
+        late = keep.tile([P, PACK - 1, N], F32, name="late", tag="codes3", align_bytes=64)
         peak(0, early[:, 0, :])
         peak(1, early[:, 1, :])
-        peak(2, late[:, 0, :])
+        peak(2, mag2[:])
         peak(3, mag3[:])
         finish(0, early[:, 2, :])
         for t in range(1, PACK):
-            finish(t, late[:, t, :])
+            finish(t, late[:, t - 1, :])
 
         y_grouped = keep.tile([P, N, PACK], BF16, name="y_grouped", align_bytes=64)
-        split = 144
         nc.vector.tensor_copy(
-            y_grouped[:, :split, :].rearrange("p (c i) t -> p c t i", i=4),
-            y[:, :, :split].rearrange("p t (c i) -> p c t i", i=4),
+            y_grouped[:, :VECTOR_COLUMNS, :].rearrange("p (c i) t -> p c t i", i=4),
+            y[:, :, :VECTOR_COLUMNS].rearrange("p t (c i) -> p c t i", i=4),
         )
         nc.scalar.copy(
-            y_grouped[:, split:, :],
-            y[:, :, split:].rearrange("p t n -> p n t"),
+            y_grouped[:, VECTOR_COLUMNS:, :],
+            y[:, :, VECTOR_COLUMNS:].rearrange("p t n -> p n t"),
         )
         y_codes = keep.tile([P, N], U32, name="y_codes", align_bytes=64)
         y_scales = keep.tile([P, N], U8, name="y_scales", align_bytes=64)
@@ -185,7 +188,7 @@ def tile_list_moment_headpicks_stored_rowpeaks_pl_kernel(tc, xf, ra, gj_words, g
             in_=y_grouped[:].rearrange("p n t -> p (n t)"),
         )
         nc.sync.dma_start(out_1[0].rearrange("p n r -> p (n r)").bitcast(I32), y_codes[:].bitcast(I32))
-        for quad in range(4):
+        for quad in range(QUADS):
             queue = nc.scalar if quad % 2 == 0 else nc.sync
             queue.dma_start(
                 out_2[0, 4 * quad : 4 * quad + 4, :].bitcast(I32),

from contextlib import ExitStack

import concourse.mybir as mybir
from concourse.masks import make_identity

K, J, N, T = 512, 512, 256, 1024
FLOPS = 2 * K * J * N

F32 = mybir.dt.float32
BF16 = mybir.dt.bfloat16
I32 = mybir.dt.int32
U32 = mybir.dt.uint32
U16 = mybir.dt.uint16
U8 = mybir.dt.uint8
E5M2X4 = mybir.dt.float8_e5m2_x4
E4M3X4 = mybir.dt.float8_e4m3fn_x4
ALU = mybir.AluOpType
ACT = mybir.ActivationFunctionType

P = 128
PACK = 4
QUADS = 4
GROUP = 16
HALF = J // 2
OLD_FACTOR = -0.3
PEAK_SHIFT = 2.0
VECTOR_COLUMNS = 192


def tile_list_moment_headpicks_stored_rowpeaks_pl_kernel(tc, xf, ra, gj_words, gj_scales, old, offs, out_0, out_1, out_2):
    nc = tc.nc
    with ExitStack() as ctx:
        keep = ctx.enter_context(tc.tile_pool(name="keep", bufs=1))
        psum = ctx.enter_context(tc.psum_pool(name="psum", bufs=1))
        turn = ctx.enter_context(tc.psum_pool(name="turn", bufs=3))

        offsets = keep.tile([P, J // GROUP], U16, name="offsets")

        xf_rows = xf.rearrange("(p t) c -> p t c", t=PACK)
        x = [keep.tile([P, T], F32, name="x%d" % t) for t in range(PACK)]
        ra4 = keep.tile([P, PACK], F32, name="ra4")
        g_words = keep.tile([P, N], U32, name="g_words", align_bytes=64)
        g_scales = keep.tile([P, N], U8, name="g_scales", align_bytes=64)
        old_sb = keep.tile([P, PACK, N], F32, name="old_sb")
        nc.gpsimd.memset(g_scales[:].bitcast(I32), 0)
        nc.scalar.dma_start(ra4[:], ra.rearrange("o (q s) -> (o q) s", s=PACK))
        nc.sync.dma_start(x[0][:], xf_rows[:, 0, :])
        nc.sync.dma_start(offsets[:], offs)
        for t in range(1, PACK):
            nc.sync.dma_start(x[t][:], xf_rows[:, t, :])
        nc.sync.dma_start(g_words[:].bitcast(I32), gj_words[0].rearrange("p n r -> p (n r)").bitcast(I32))
        for quad in range(QUADS):
            nc.sync.dma_start(
                g_scales[32 * quad : 32 * quad + 4, :].bitcast(I32),
                gj_scales[0, 4 * quad : 4 * quad + 4, :].bitcast(I32),
            )
        nc.sync.dma_start(old_sb[:], old.rearrange("(p t) n -> p t n", t=PACK))

        ident = keep.tile([P, P], F32, name="ident")
        make_identity(nc, ident[:])
        one = keep.tile([P, 1], F32, name="one")
        shift = keep.tile([P, 1], F32, name="shift")
        nc.gpsimd.memset(one[:], 1.0)
        nc.scalar.activation(shift[:], one[:], ACT.Abs, scale=PEAK_SHIFT)

        ra_all = psum.tile([P, PACK, P], F32, name="ra_all")
        for s in range(PACK):
            nc.tensor.transpose(ra_all[:, s, :], ra4[:, s : s + 1].to_broadcast([P, P]), ident[:])

        picked0 = keep.tile([P, J], F32, name="picked0")
        picked1_hi = keep.tile([P, HALF], F32, name="picked1_hi")
        picked2 = keep.tile([P, J], F32, name="picked2")
        picked3_lo = keep.tile([P, HALF], F32, name="picked3_lo")
        picked3_hi = keep.tile([P, HALF], F32, name="picked3_hi", align_bytes=64)
        u_scales = [keep.tile([P, P], U8, name="u_scales%d" % t, align_bytes=64) for t in range(PACK)]
        w = [psum.tile([P, N], F32, name="w%d" % t) for t in range(PACK)]
        denom = [keep.tile([P, 1], F32, name="denom%d" % t) for t in range(PACK)]
        inv = [keep.tile([P, 1], F32, name="inv%d" % t) for t in range(PACK)]
        y = keep.tile([P, PACK, N], F32, name="y")
        out_rows = out_0.rearrange("(p t) n -> p t n", t=PACK)
        lo_list = offsets[:, : HALF // GROUP]
        hi_list = offsets[:, HALF // GROUP :]

        def weigh(pairs, values, q0, q1):
            nc.vector.tensor_tensor(
                pairs[:, :, q0:q1, :],
                values.rearrange("p (q u e) -> p u q e", u=2, e=2),
                ra_all[:].rearrange("p (u e) q -> p u q e", u=2)[:, :, q0:q1, :],
                ALU.mult,
            )

        def turn_over(pairs, grouped, copy):
            words = pairs[:].rearrange("p u q e -> p (u q e)").bitcast(F32)
            turned = turn.tile([P, 2, P], F32, name="turned")
            for u in range(2):
                nc.tensor.transpose(turned[:, u, :], words[:, u * P : (u + 1) * P], ident[:])
            dst = grouped[:].rearrange("q p s -> q (p s)").bitcast(F32).rearrange("q (p u) -> q p u", u=2)
            copy(dst, turned[:].rearrange("q u p -> q p u"))

        def product(t, grouped, codes):
            nc.vector.quantize_mx(
                out=codes.bitcast(E5M2X4),
                scales=u_scales[t][:],
                in_=grouped[:].rearrange("q p s -> q (p s)"),
            )
            nc.tensor.matmul_mx(
                out=w[t][:],
                lhsT=codes.bitcast(E5M2X4),
                lhsT_scale=u_scales[t][:],
                rhs=g_words[:].bitcast(E5M2X4),
                rhs_scale=g_scales[:],
                start=True,
                stop=True,
            )

        def peak(t, mag):
            nc.scalar.activation(mag, w[t][:], ACT.Abs)
            nc.vector.tensor_scalar(mag, mag, shift[:], None, ALU.add, ALU.max, accum_out=denom[t][:])
            nc.vector.reciprocal(inv[t][:], denom[t][:])

        def finish(t, part):
            nc.scalar.activation(part, old_sb[:, t, :], ACT.Copy, scale=OLD_FACTOR)
            nc.vector.scalar_tensor_tensor(y[:, t, :], w[t][:], inv[t][:], part, ALU.mult, ALU.add)
            nc.sync.dma_start(out_rows[:, t, :], y[:, t, :])

        def pair_tile(t, tag):
            return keep.tile([P, 2, P, 2], BF16, name="pairs%d" % t, tag=tag, align_bytes=64)

        grouped = [keep.tile([P, P, PACK], BF16, name="grouped%d" % t, align_bytes=64) for t in range(PACK)]

        nc.vector.tensor_copy(picked0[:, :HALF], x[0][:].indirect(lo_list))
        nc.scalar.activation(picked0[:, HALF:], x[0][:].indirect(hi_list), ACT.Copy)
        nc.scalar.activation(picked1_hi[:], x[1][:].indirect(hi_list), ACT.Copy)
        nc.scalar.activation(picked2[:], x[2][:].indirect(offsets[:]), ACT.Copy)
        nc.scalar.activation(picked3_lo[:], x[3][:].indirect(lo_list), ACT.Copy)
        nc.scalar.activation(picked3_hi[:], x[3][:].indirect(hi_list), ACT.Copy)

        pairs0 = pair_tile(0, "pairs0")
        weigh(pairs0, picked0[:], 0, P)
        picked1_lo = keep.tile([P, HALF], F32, name="picked1_lo", tag="picked0")
        nc.vector.tensor_copy(picked1_lo[:], x[1][:].indirect(lo_list))
        pairs1 = pair_tile(1, "pairs1")
        weigh(pairs1, picked1_hi[:], P // 2, P)
        weigh(pairs1, picked1_lo[:], 0, P // 2)
        turn_over(pairs0, grouped[0], nc.vector.tensor_copy)
        pairs2 = pair_tile(2, "pairs0")
        weigh(pairs2, picked2[:], 0, P)
        turn_over(pairs1, grouped[1], nc.scalar.copy)
        pairs3 = pair_tile(3, "pairs1")
        weigh(pairs3, picked3_lo[:], 0, P // 2)
        codes0 = keep.tile([P, P], U32, name="codes0", align_bytes=64)
        product(0, grouped[0], codes0[:])
        weigh(pairs3, picked3_hi[:], P // 2, P)
        turn_over(pairs2, grouped[2], nc.scalar.copy)
        turn_over(pairs3, grouped[3], nc.scalar.copy)
        codes3 = keep.tile([P, P], U32, name="codes3", align_bytes=64)
        product(3, grouped[3], codes3[:])
        codes12 = keep.tile([P, 2, P], U32, name="codes12", tag="picked3_hi", align_bytes=64)
        product(1, grouped[1], codes12[:, 0, :])
        product(2, grouped[2], codes12[:, 1, :])

        early = keep.tile([P, 3, N], F32, name="early", tag="picked3_lo")
        mag2 = keep.tile([P, N], F32, name="mag2", tag="pairs1", align_bytes=64)
        mag3 = keep.tile([P, N], F32, name="mag3")
        late = keep.tile([P, PACK - 1, N], F32, name="late", tag="codes3", align_bytes=64)
        peak(0, early[:, 0, :])
        peak(1, early[:, 1, :])
        peak(2, mag2[:])
        peak(3, mag3[:])
        finish(0, early[:, 2, :])
        for t in range(1, PACK):
            finish(t, late[:, t - 1, :])

        y_grouped = keep.tile([P, N, PACK], BF16, name="y_grouped", align_bytes=64)
        nc.vector.tensor_copy(
            y_grouped[:, :VECTOR_COLUMNS, :].rearrange("p (c i) t -> p c t i", i=4),
            y[:, :, :VECTOR_COLUMNS].rearrange("p t (c i) -> p c t i", i=4),
        )
        nc.scalar.copy(
            y_grouped[:, VECTOR_COLUMNS:, :],
            y[:, :, VECTOR_COLUMNS:].rearrange("p t n -> p n t"),
        )
        y_codes = keep.tile([P, N], U32, name="y_codes", align_bytes=64)
        y_scales = keep.tile([P, N], U8, name="y_scales", align_bytes=64)
        nc.vector.quantize_mx(
            out=y_codes[:].bitcast(E4M3X4),
            scales=y_scales[:],
            in_=y_grouped[:].rearrange("p n t -> p (n t)"),
        )
        nc.sync.dma_start(out_1[0].rearrange("p n r -> p (n r)").bitcast(I32), y_codes[:].bitcast(I32))
        for quad in range(QUADS):
            queue = nc.scalar if quad % 2 == 0 else nc.sync
            queue.dma_start(
                out_2[0, 4 * quad : 4 * quad + 4, :].bitcast(I32),
                y_scales[32 * quad : 32 * quad + 4, :].bitcast(I32),
            )
